import numpy as np
import ml_dtypes


def mxq(x, axis, fmt="e4m3"):
    dtype, down = {"e4m3": (ml_dtypes.float8_e4m3fn, 7), "e5m2": (ml_dtypes.float8_e5m2, 14)}[fmt]
    v = np.moveaxis(np.asarray(x, np.float32).astype(ml_dtypes.bfloat16).astype(np.float64), axis, -1)
    blocks = v.reshape(v.shape[:-1] + (-1, 32))
    amax = np.abs(blocks).max(-1, keepdims=True)
    byte = np.maximum(np.where(amax > 0, np.frexp(amax)[1] - 1 + 127, 0) - down, 1)
    scale = np.exp2(byte - 127.0)
    codes = (blocks / scale).astype(np.float32).astype(dtype).astype(np.float64)
    return np.moveaxis((codes * scale).reshape(v.shape), -1, axis)


WIDE = False


def mx_kscale(k):
    if not WIDE:
        return np.ones(k)
    levels = np.array([18, -18])
    if k % 512:
        return np.exp2(np.random.permutation(np.resize(levels, k // 32))).repeat(32)
    a = np.empty((k // 512, 16))
    for p in range(k // 512):
        a[p, :8] = np.random.permutation(np.resize(levels, 8))
        for g in range(8):
            far = levels[np.abs(levels - a[p, g]) >= 10]
            a[p, g + 8] = far[np.random.randint(len(far))]
    return np.exp2(a.ravel()).repeat(32)


def f64(x):
    return np.asarray(x).astype(np.float64)


def striped(idx):
    return np.tile(np.asarray(idx).reshape(-1, 16).T, (8, 1)).astype(np.uint16)


def unstriped(offs):
    return offs[:16].T.reshape(-1).astype(np.int64)

def planes(y):
    n, m = y.shape
    v = y.astype(np.float32).astype(ml_dtypes.bfloat16).astype(np.float64).reshape(n // 32, 32, m)
    top = np.abs(v).max(1)
    byte = np.clip(np.where(top > 0, np.frexp(top)[1] - 1 + 127 - 7, 1), 1, 254)
    codes = (v * np.exp2(127.0 - byte)[:, None, :]).reshape(n, m).astype(np.float32).astype(ml_dtypes.float8_e4m3fn).view(np.uint8)
    words = codes.reshape(n // 512, 128, 4, m).transpose(0, 1, 3, 2)
    return np.ascontiguousarray(words), np.ascontiguousarray(byte.astype(np.uint8).reshape(n // 512, 16, m))


def setup_inputs():
    n = np.random.standard_normal
    uni = np.random.uniform
    idx = np.random.permutation(2048)[:512]
    f_r = mx_kscale(512)
    return {
        "xT": (n((512, 512)) * f_r[None, :]).astype(np.float32),
        "G": (n((512, 512)) / np.sqrt(512) / f_r[:, None]).astype(np.float32),
        "mT": (0.3 * n((512, 2048))).astype(np.float32),
        "v": np.tile(uni(0.5, 1.5, 2048), (128, 1)).astype(np.float32),
        "offs": striped(idx),
    }


def reference(xT, G, mT, v, offs):
    idx = unstriped(offs)
    m = f64(mT)[:, idx]
    v_i = f64(v)[:1][:, idx]
    dw = mxq(f64(xT), 1, "e4m3") @ mxq(f64(G), 0, "e5m2")
    dt = dw.T
    q = (np.square(dt)).sum(-1, keepdims=True)
    qr = q.T
    nv = 0.99 * v_i + 0.01 * qr / 512.0
    nm = 0.9 * m + 0.1 * dw
    up = nm / (np.sqrt(nv) + 0.001)
    out_0 = np.zeros((512, 2048))
    out_0[:, idx] = up
    out_1 = np.zeros((512, 2048))
    out_1[:, idx] = nm
    nvc = nv.T
    out_2 = nvc.T
    return (out_0, out_1, out_2,) + planes(out_0)

@@ -1,0 +1,250 @@
+from contextlib import ExitStack
+import math
+
+import concourse.mybir as mybir
+from concourse.masks import make_identity
+
+F32 = mybir.dt.float32
+BF16 = mybir.dt.bfloat16
+U32 = mybir.dt.uint32
+I32 = mybir.dt.int32
+U16 = mybir.dt.uint16
+U8 = mybir.dt.uint8
+E4M3 = mybir.dt.float8_e4m3fn_x4
+E5M2 = mybir.dt.float8_e5m2_x4
+ACT = mybir.ActivationFunctionType
+ALU = mybir.AluOpType
+
+P = 128
+PACK = 4
+D = 512
+R = 512
+SLOTS = 512
+COLS = 2048
+PIECE = 512
+RUN = 4
+
+BETA1 = 0.9
+BETA2 = 0.99
+EPS = 0.001
+DW_SCALE = (1.0 - BETA1) / BETA1
+TINY = 1e-30
+
+FLOPS = 2 * D * R * SLOTS
+BYTES = 4 * (D * R + R * SLOTS + D * COLS + COLS + 2 * D * COLS + SLOTS) + 2 * P * SLOTS // 16 + D * COLS + 16 * COLS
+
+
+def tile_attend_grwadam_pl_kernel(tc, xT, G, mT, v, offs, out_0, out_1, out_2, out_3, out_4):
+    nc = tc.nc
+    blocks = SLOTS // P
+    pieces = COLS // PIECE
+
+    x_rows = xT.rearrange("(p t) r -> t p r", t=PACK)
+    m_rows = mT.rearrange("(p t) c -> t p c", t=PACK)
+    up_rows = out_0.rearrange("(p t) c -> t p c", t=PACK)
+    nm_rows = out_1.rearrange("(p t) c -> t p c", t=PACK)
+
+    with ExitStack() as ctx:
+        keep = ctx.enter_context(tc.tile_pool(name="keep", bufs=1))
+        wide = ctx.enter_context(tc.tile_pool(name="wide", bufs=PACK))
+        turn_ps = ctx.enter_context(tc.psum_pool(name="turn_ps", bufs=2))
+        dw_ps = ctx.enter_context(tc.psum_pool(name="dw_ps", bufs=2))
+        sq_ps = ctx.enter_context(tc.psum_pool(name="sq_ps", bufs=1))
+
+        offsets = keep.tile([P, SLOTS // 16], U16, name="offsets")
+        nc.sync.dma_start(offsets[:], offs)
+
+        v_row = keep.tile([P, COLS // P], F32, name="v_row")
+        nc.sync.dma_start(out=v_row[:], in_=v[0].rearrange("(p j) -> p j", p=P))
+        g_raw = keep.tile([P, PACK, SLOTS], F32, name="g_raw")
+        nc.sync.dma_start(out=g_raw[:], in_=G.rearrange("(p j) i -> p j i", j=PACK))
+        x_raw = []
+        for t in range(PACK):
+            tile = keep.tile([P, R], F32, name=f"x_raw{t}")
+            nc.sync.dma_start(out=tile[:], in_=x_rows[t])
+            x_raw.append(tile)
+        m_table = []
+        for t in range(PACK):
+            tile = wide.tile([P, COLS], F32, name=f"m_table{t}", tag="wide")
+            nc.sync.dma_start(out=tile[:], in_=m_rows[t])
+            m_table.append(tile)
+
+        nm_windows = [keep.tile([P, COLS], F32, name="nm_window0")]
+        up_windows = [keep.tile([P, COLS], F32, name=f"up_window{k}") for k in range(2)]
+        nc.vector.memset(nm_windows[0][:], 0.0)
+        nc.vector.memset(up_windows[0][:], 0.0)
+
+        ident = keep.tile([P, P], F32, name="ident")
+        make_identity(nc, ident[:])
+        one = keep.tile([P, 1], F32, name="one")
+        nc.gpsimd.memset(one[:], 1.0)
+        nv_cols = keep.tile([P, P], F32, name="nv_cols")
+        nc.gpsimd.memset(nv_cols[:], 0.0)
+        nc.gpsimd.memset(up_windows[1][:], 0.0)
+
+        warm = keep.tile([P, 1], F32, name="warm")
+        nc.scalar.activation(out=warm[:], in_=one[:], func=ACT.Abs_reciprocal_sqrt)
+        beta_early = keep.tile([P, SLOTS], F32, name="beta_early")
+        nc.scalar.activation(out=beta_early[:], in_=one[:].to_broadcast([P, SLOTS]), func=ACT.Copy, scale=BETA1)
+
+        v_table = keep.tile([P, COLS], F32, name="v_table")
+        v_lines = v_table[:].rearrange("m (p a j) -> m a p j", a=blocks, j=RUN)
+        for a in range(blocks):
+            spread = sq_ps.tile([P, RUN, P], F32, name=f"spread{a}", tag=f"bank{a}")
+            for j in range(RUN):
+                column = v_row[:, RUN * a + j : RUN * a + j + 1]
+                nc.tensor.transpose(spread[:, j, :], column.to_broadcast([P, P]), ident[:])
+            nc.scalar.copy(out=v_lines[:, a], in_=spread[:].rearrange("m j p -> m p j"))
+
+        g_bf = keep.tile([P, SLOTS, PACK], BF16, name="g_bf", align_bytes=64)
+        nc.vector.tensor_copy(
+            out=g_bf[:].rearrange("p (c i) j -> p c j i", i=RUN),
+            in_=g_raw[:].rearrange("p j (c i) -> p c j i", i=RUN),
+        )
+        g_codes = keep.tile([P, SLOTS], U32, name="g_codes", align_bytes=64)
+        g_scales = keep.tile([P, SLOTS], U8, name="g_scales", align_bytes=64)
+        nc.vector.quantize_mx(
+            out=g_codes[:].bitcast(E5M2), scales=g_scales[:], in_=g_bf[:].rearrange("p i j -> p (i j)")
+        )
+
+        v_listed = keep.tile([P, SLOTS], F32, name="v_listed")
+        nc.vector.tensor_copy(v_listed[:], v_table[:].indirect(offsets[:]))
+
+        shared = keep.tile([P, 2 * SLOTS], F32, name="shared")
+        dw9 = [keep.tile([P, SLOTS], F32, name=f"dw9_{t}")[:] for t in range(PACK - 1)] + [shared[:, :SLOTS]]
+        moment = [shared[:, SLOTS:]] + [keep.tile([P, SLOTS], F32, name=f"moment{t}")[:] for t in range(1, PACK)]
+        beta_late = shared[:, SLOTS // 2 : SLOTS // 2 + SLOTS]
+
+        turned = [sq_ps.tile([P, PACK, P], F32, name=f"turned{b}", tag=f"bank{b}") for b in range(blocks)]
+
+        for t in range(PACK):
+            x_bf = keep.tile([P, 2, P, 2], BF16, name=f"x_bf{t}")
+            cast = nc.scalar.copy if t < 3 else nc.vector.tensor_copy
+            cast(out=x_bf[:], in_=x_raw[t][:].rearrange("m (p u e) -> m u p e", u=2, e=2))
+            x_words = x_bf[:].rearrange("m u p e -> m (u p e)").bitcast(F32)
+            x_turned = turn_ps.tile([P, 2, P], F32, name="x_turned", tag="turn")
+            for u in range(2):
+                nc.tensor.transpose(x_turned[:, u, :], x_words[:, u * P : (u + 1) * P], ident[:])
+            x_grouped = keep.tile([P, P * PACK], BF16, name=f"x_grouped{t}", align_bytes=64)
+            nc.scalar.copy(
+                out=x_grouped[:].bitcast(F32).rearrange("p (m u) -> p m u", u=2),
+                in_=x_turned[:].rearrange("p u m -> p m u"),
+            )
+            x_codes = keep.tile([P, P], U32, name=f"x_codes{t}", align_bytes=64)
+            x_scales = keep.tile([P, P], U8, name=f"x_scales{t}", align_bytes=64)
+            nc.vector.quantize_mx(out=x_codes[:].bitcast(E4M3), scales=x_scales[:], in_=x_grouped[:])
+            dw = dw_ps.tile([P, SLOTS], F32, name="dw", tag="dw")
+            nc.tensor.matmul_mx(
+                out=dw[:],
+                lhsT=x_codes[:].bitcast(E4M3),
+                lhsT_scale=x_scales[:],
+                rhs=g_codes[:].bitcast(E5M2),
+                rhs_scale=g_scales[:],
+                start=True,
+                stop=True,
+            )
+            nc.scalar.activation(out=dw9[t], in_=dw[:], func=ACT.Copy, scale=DW_SCALE)
+            for b in range(blocks):
+                nc.tensor.transpose(turned[b][:, t, :], dw9[t][:, b * P : (b + 1) * P], ident[:])
+
+        def gather_moment(t):
+            nc.vector.tensor_tensor(moment[t], m_table[t][:].indirect(offsets[:]), dw9[t], ALU.add)
+
+        def scatter_moment(t, window, beta):
+            nc.vector.tensor_tensor(window[:].indirect(offsets[:]), moment[t], beta, ALU.mult)
+            nc.sync.dma_start(out=nm_rows[t], in_=window[:])
+
+        def late_window(name):
+            window = wide.tile([P, COLS], F32, name=name, tag="wide")
+            nc.gpsimd.memset(window[:], 0.0)
+            return window
+
+        gather_moment(0)
+        scatter_moment(0, nm_windows[0], beta_early[:])
+
+        v_turned = turn_ps.tile([P, blocks, P], F32, name="v_turned", tag="turn")
+        for b in range(blocks):
+            nc.tensor.transpose(v_turned[:, b, :], v_listed[:, b * P : (b + 1) * P], ident[:])
+        v_cols = keep.tile([P, blocks], F32, name="v_cols")
+        nc.scalar.activation(out=v_cols[:], in_=v_turned[:, :, 0], func=ACT.Copy, scale=BETA2)
+
+        q_cols = keep.tile([P, blocks], F32, name="q_cols")
+        squares = keep.tile([P, D], F32, name="squares")
+        rsqrt = keep.tile([P, blocks], F32, name="rsqrt")
+        denom2 = keep.tile([P, blocks], F32, name="denom2")
+        rate_cols = keep.tile([P, blocks], F32, name="rate_cols")
+        sq_scale = math.sqrt((1.0 - BETA2) / D) / DW_SCALE
+        for b in range(blocks):
+            col = slice(b, b + 1)
+            nc.scalar.activation(
+                out=squares[:],
+                in_=turned[b][:].rearrange("i t p -> i (t p)"),
+                func=ACT.Square,
+                scale=sq_scale,
+                accum_out=q_cols[:, col],
+            )
+            nc.scalar.activation(out=nv_cols[:, col], in_=q_cols[:, col], func=ACT.Identity, bias=v_cols[:, col])
+        nc.scalar.activation(out=rsqrt[:], in_=nv_cols[:, :blocks], func=ACT.Abs_reciprocal_sqrt, bias=TINY)
+        for b in range(blocks):
+            col = slice(b, b + 1)
+            nc.scalar.activation(
+                out=denom2[:, col], in_=nv_cols[:, col], func=ACT.Square, scale=rsqrt[:, col], bias=EPS
+            )
+        nc.scalar.activation(
+            out=rate_cols[:], in_=denom2[:], func=ACT.Abs_reciprocal_sqrt, scale=1.0 / (BETA1 * BETA1)
+        )
+        rate_ps = turn_ps.tile([P, blocks, P], F32, name="rate_ps", tag="turn")
+        for b in range(blocks):
+            nc.tensor.transpose(rate_ps[:, b, :], rate_cols[:, b : b + 1].to_broadcast([P, P]), ident[:])
+        rate = keep.tile([P, SLOTS], F32, name="rate")
+        nc.scalar.copy(out=rate[:], in_=rate_ps[:].rearrange("p b i -> p (b i)"))
+
+        nv_ps = turn_ps.tile([P, P], F32, name="nv_ps", tag="turn")
+        nc.tensor.transpose(nv_ps[:], nv_cols[:], ident[:])
+        nv_rows = keep.tile([32, P], F32, name="nv_rows")
+        nc.scalar.copy(out=nv_rows[:], in_=nv_ps[0:32, :])
+        nc.sync.dma_start(out=out_2.rearrange("o (b i) -> (o b) i", b=blocks), in_=nv_rows[0:blocks, :])
+
+        for t in range(1, PACK):
+            gather_moment(t)
+        up_windows.append(late_window("up_window2"))
+        up_windows.append(late_window("up_window3"))
+        nm_windows.append(late_window("nm_window1"))
+        nm_windows.append(late_window("nm_window2"))
+
+        rounded = [keep.tile([P, PACK, PIECE], BF16, name=f"rounded{k}") for k in range(pieces)]
+        grouped = [keep.tile([P, PIECE, PACK], BF16, name=f"grouped{k}", align_bytes=64) for k in range(pieces)]
+        for t in range(PACK):
+            window = up_windows[t % len(up_windows)]
+            nc.vector.tensor_tensor(window[:].indirect(offsets[:]), moment[t], rate[:], ALU.mult)
+            nc.sync.dma_start(out=up_rows[t], in_=window[:])
+            if t == 0:
+                nc.scalar.activation(out=beta_late, in_=one[:].to_broadcast([P, SLOTS]), func=ACT.Copy, scale=BETA1)
+            for k in range(pieces):
+                nc.scalar.copy(out=rounded[k][:, t, :], in_=window[:, k * PIECE : (k + 1) * PIECE])
+                if t == PACK - 1:
+                    nc.scalar.copy(
+                        out=grouped[k][:].rearrange("p (c i) t -> p c t i", i=RUN),
+                        in_=rounded[k][:].rearrange("p t (c i) -> p c t i", i=RUN),
+                    )
+
+        for t in range(1, PACK):
+            scatter_moment(t, nm_windows[t - 1], beta_late)
+
+        up_codes = keep.tile([P, COLS], U32, name="up_codes", align_bytes=64)
+        up_scales = keep.tile([P, COLS], U8, name="up_scales", align_bytes=64)
+        words = out_3[0].rearrange("p c j -> p (c j)").bitcast(I32)
+        for k in range(pieces):
+            cols = slice(k * PIECE, (k + 1) * PIECE)
+            nc.vector.quantize_mx(
+                out=up_codes[:, cols].bitcast(E4M3),
+                scales=up_scales[:, cols],
+                in_=grouped[k][:].rearrange("p c t -> p (c t)"),
+            )
+            nc.sync.dma_start(out=words[:, cols], in_=up_codes[:, cols].bitcast(I32))
+        scale_rows = out_4[0].bitcast(I32)
+        for quad in range(4):
+            nc.scalar.dma_start(
+                out=scale_rows[4 * quad : 4 * quad + 4, :],
+                in_=up_scales[32 * quad : 32 * quad + 4, :].bitcast(I32),
+            )

@@ -46,7 +46,6 @@ def tile_attend_grwadam_pl_kernel(tc, xT, G, mT, v, offs, out_0, out_1, out_2, o
 
     with ExitStack() as ctx:
         keep = ctx.enter_context(tc.tile_pool(name="keep", bufs=1))
-        wide = ctx.enter_context(tc.tile_pool(name="wide", bufs=PACK))
         turn_ps = ctx.enter_context(tc.psum_pool(name="turn_ps", bufs=2))
         dw_ps = ctx.enter_context(tc.psum_pool(name="dw_ps", bufs=2))
         sq_ps = ctx.enter_context(tc.psum_pool(name="sq_ps", bufs=1))
@@ -56,23 +55,22 @@ def tile_attend_grwadam_pl_kernel(tc, xT, G, mT, v, offs, out_0, out_1, out_2, o
 
         v_row = keep.tile([P, COLS // P], F32, name="v_row")
         nc.sync.dma_start(out=v_row[:], in_=v[0].rearrange("(p j) -> p j", p=P))
+        x_raw = [keep.tile([P, R], F32, name=f"x_raw{t}") for t in range(PACK)]
         g_raw = keep.tile([P, PACK, SLOTS], F32, name="g_raw")
+        nc.sync.dma_start(out=x_raw[0][:], in_=x_rows[0])
         nc.sync.dma_start(out=g_raw[:], in_=G.rearrange("(p j) i -> p j i", j=PACK))
-        x_raw = []
-        for t in range(PACK):
-            tile = keep.tile([P, R], F32, name=f"x_raw{t}")
-            nc.sync.dma_start(out=tile[:], in_=x_rows[t])
-            x_raw.append(tile)
+        for t in range(1, PACK):
+            nc.sync.dma_start(out=x_raw[t][:], in_=x_rows[t])
         m_table = []
         for t in range(PACK):
-            tile = wide.tile([P, COLS], F32, name=f"m_table{t}", tag="wide")
+            tile = keep.tile([P, COLS], F32, name=f"m_table{t}")
             nc.sync.dma_start(out=tile[:], in_=m_rows[t])
             m_table.append(tile)
 
-        nm_windows = [keep.tile([P, COLS], F32, name="nm_window0")]
-        up_windows = [keep.tile([P, COLS], F32, name=f"up_window{k}") for k in range(2)]
-        nc.vector.memset(nm_windows[0][:], 0.0)
-        nc.vector.memset(up_windows[0][:], 0.0)
+        nm_windows = [keep.tile([P, COLS], F32, name=f"nm_window{k}") for k in range(2)]
+        up_windows = [keep.tile([P, COLS], F32, name=f"up_window{k}") for k in range(3)]
+        for window in nm_windows + up_windows:
+            nc.vector.memset(window[:].bitcast(I32), 0)
 
         ident = keep.tile([P, P], F32, name="ident")
         make_identity(nc, ident[:])
@@ -80,12 +78,14 @@ def tile_attend_grwadam_pl_kernel(tc, xT, G, mT, v, offs, out_0, out_1, out_2, o
         nc.gpsimd.memset(one[:], 1.0)
         nv_cols = keep.tile([P, P], F32, name="nv_cols")
         nc.gpsimd.memset(nv_cols[:], 0.0)
-        nc.gpsimd.memset(up_windows[1][:], 0.0)
 
         warm = keep.tile([P, 1], F32, name="warm")
         nc.scalar.activation(out=warm[:], in_=one[:], func=ACT.Abs_reciprocal_sqrt)
-        beta_early = keep.tile([P, SLOTS], F32, name="beta_early")
-        nc.scalar.activation(out=beta_early[:], in_=one[:].to_broadcast([P, SLOTS]), func=ACT.Copy, scale=BETA1)
+        factors = keep.tile([P, 2 * SLOTS], F32, name="factors")
+        rate = factors[:, :SLOTS]
+        beta_early = factors[:, SLOTS:]
+        beta_late = factors[:, SLOTS - 1 : 2 * SLOTS - 1]
+        nc.scalar.activation(out=beta_early, in_=one[:].to_broadcast([P, SLOTS]), func=ACT.Copy, scale=BETA1)
 
         v_table = keep.tile([P, COLS], F32, name="v_table")
         v_lines = v_table[:].rearrange("m (p a j) -> m a p j", a=blocks, j=RUN)
@@ -110,10 +110,8 @@ def tile_attend_grwadam_pl_kernel(tc, xT, G, mT, v, offs, out_0, out_1, out_2, o
         v_listed = keep.tile([P, SLOTS], F32, name="v_listed")
         nc.vector.tensor_copy(v_listed[:], v_table[:].indirect(offsets[:]))
 
-        shared = keep.tile([P, 2 * SLOTS], F32, name="shared")
-        dw9 = [keep.tile([P, SLOTS], F32, name=f"dw9_{t}")[:] for t in range(PACK - 1)] + [shared[:, :SLOTS]]
-        moment = [shared[:, SLOTS:]] + [keep.tile([P, SLOTS], F32, name=f"moment{t}")[:] for t in range(1, PACK)]
-        beta_late = shared[:, SLOTS // 2 : SLOTS // 2 + SLOTS]
+        dw9 = [keep.tile([P, SLOTS], F32, name=f"dw9_{t}")[:] for t in range(PACK)]
+        moment = [keep.tile([P, SLOTS], F32, name=f"moment{t}")[:] for t in range(PACK)]
 
         turned = [sq_ps.tile([P, PACK, P], F32, name=f"turned{b}", tag=f"bank{b}") for b in range(blocks)]
 
@@ -154,13 +152,8 @@ def tile_attend_grwadam_pl_kernel(tc, xT, G, mT, v, offs, out_0, out_1, out_2, o
             nc.vector.tensor_tensor(window[:].indirect(offsets[:]), moment[t], beta, ALU.mult)
             nc.sync.dma_start(out=nm_rows[t], in_=window[:])
 
-        def late_window(name):
-            window = wide.tile([P, COLS], F32, name=name, tag="wide")
-            nc.gpsimd.memset(window[:], 0.0)
-            return window
-
         gather_moment(0)
-        scatter_moment(0, nm_windows[0], beta_early[:])
+        scatter_moment(0, nm_windows[0], beta_early)
 
         v_turned = turn_ps.tile([P, blocks, P], F32, name="v_turned", tag="turn")
         for b in range(blocks):
@@ -196,8 +189,7 @@ def tile_attend_grwadam_pl_kernel(tc, xT, G, mT, v, offs, out_0, out_1, out_2, o
         rate_ps = turn_ps.tile([P, blocks, P], F32, name="rate_ps", tag="turn")
         for b in range(blocks):
             nc.tensor.transpose(rate_ps[:, b, :], rate_cols[:, b : b + 1].to_broadcast([P, P]), ident[:])
-        rate = keep.tile([P, SLOTS], F32, name="rate")
-        nc.scalar.copy(out=rate[:], in_=rate_ps[:].rearrange("p b i -> p (b i)"))
+        nc.scalar.copy(out=rate, in_=rate_ps[:].rearrange("p b i -> p (b i)"))
 
         nv_ps = turn_ps.tile([P, P], F32, name="nv_ps", tag="turn")
         nc.tensor.transpose(nv_ps[:], nv_cols[:], ident[:])
@@ -207,19 +199,13 @@ def tile_attend_grwadam_pl_kernel(tc, xT, G, mT, v, offs, out_0, out_1, out_2, o
 
         for t in range(1, PACK):
             gather_moment(t)
-        up_windows.append(late_window("up_window2"))
-        up_windows.append(late_window("up_window3"))
-        nm_windows.append(late_window("nm_window1"))
-        nm_windows.append(late_window("nm_window2"))
 
         rounded = [keep.tile([P, PACK, PIECE], BF16, name=f"rounded{k}") for k in range(pieces)]
         grouped = [keep.tile([P, PIECE, PACK], BF16, name=f"grouped{k}", align_bytes=64) for k in range(pieces)]
         for t in range(PACK):
             window = up_windows[t % len(up_windows)]
-            nc.vector.tensor_tensor(window[:].indirect(offsets[:]), moment[t], rate[:], ALU.mult)
+            nc.vector.tensor_tensor(window[:].indirect(offsets[:]), moment[t], rate, ALU.mult)
             nc.sync.dma_start(out=up_rows[t], in_=window[:])
-            if t == 0:
-                nc.scalar.activation(out=beta_late, in_=one[:].to_broadcast([P, SLOTS]), func=ACT.Copy, scale=BETA1)
             for k in range(pieces):
                 nc.scalar.copy(out=rounded[k][:, t, :], in_=window[:, k * PIECE : (k + 1) * PIECE])
                 if t == PACK - 1:
@@ -228,8 +214,9 @@ def tile_attend_grwadam_pl_kernel(tc, xT, G, mT, v, offs, out_0, out_1, out_2, o
                         in_=rounded[k][:].rearrange("p t (c i) -> p c t i", i=RUN),
                     )
 
+        nc.vector.tensor_copy(out=beta_late[:, 0:1], in_=beta_early[:, 0:1])
         for t in range(1, PACK):
-            scatter_moment(t, nm_windows[t - 1], beta_late)
+            scatter_moment(t, nm_windows[t % len(nm_windows)], beta_late)
 
         up_codes = keep.tile([P, COLS], U32, name="up_codes", align_bytes=64)
         up_scales = keep.tile([P, COLS], U8, name="up_scales", align_bytes=64)

@@ -46,6 +46,7 @@ def tile_attend_grwadam_pl_kernel(tc, xT, G, mT, v, offs, out_0, out_1, out_2, o
 
     with ExitStack() as ctx:
         keep = ctx.enter_context(tc.tile_pool(name="keep", bufs=1))
+        wide = ctx.enter_context(tc.tile_pool(name="wide", bufs=PACK))
         turn_ps = ctx.enter_context(tc.psum_pool(name="turn_ps", bufs=2))
         dw_ps = ctx.enter_context(tc.psum_pool(name="dw_ps", bufs=2))
         sq_ps = ctx.enter_context(tc.psum_pool(name="sq_ps", bufs=1))
@@ -56,21 +57,22 @@ def tile_attend_grwadam_pl_kernel(tc, xT, G, mT, v, offs, out_0, out_1, out_2, o
         v_row = keep.tile([P, COLS // P], F32, name="v_row")
         nc.sync.dma_start(out=v_row[:], in_=v[0].rearrange("(p j) -> p j", p=P))
         x_raw = [keep.tile([P, R], F32, name=f"x_raw{t}") for t in range(PACK)]
-        g_raw = keep.tile([P, PACK, SLOTS], F32, name="g_raw")
-        nc.sync.dma_start(out=x_raw[0][:], in_=x_rows[0])
-        nc.sync.dma_start(out=g_raw[:], in_=G.rearrange("(p j) i -> p j i", j=PACK))
-        for t in range(1, PACK):
+        for t in range(PACK):
             nc.sync.dma_start(out=x_raw[t][:], in_=x_rows[t])
+        g_rows = G.rearrange("(p j) (h i) -> h p j i", j=PACK, h=2)
+        g_raw = [keep.tile([P, PACK, SLOTS // 2], F32, name=f"g_raw{h}") for h in range(2)]
+        for h in range(2):
+            nc.sync.dma_start(out=g_raw[h][:], in_=g_rows[h])
         m_table = []
         for t in range(PACK):
-            tile = keep.tile([P, COLS], F32, name=f"m_table{t}")
+            tile = wide.tile([P, COLS], F32, name=f"m_table{t}", tag="wide")
             nc.sync.dma_start(out=tile[:], in_=m_rows[t])
             m_table.append(tile)
 
-        nm_windows = [keep.tile([P, COLS], F32, name=f"nm_window{k}") for k in range(2)]
-        up_windows = [keep.tile([P, COLS], F32, name=f"up_window{k}") for k in range(3)]
-        for window in nm_windows + up_windows:
-            nc.vector.memset(window[:].bitcast(I32), 0)
+        nm_windows = [keep.tile([P, COLS], F32, name="nm_window0")]
+        up_windows = [keep.tile([P, COLS], F32, name=f"up_window{k}") for k in range(2)]
+        nc.vector.memset(nm_windows[0][:], 0.0)
+        nc.vector.memset(up_windows[0][:], 0.0)
 
         ident = keep.tile([P, P], F32, name="ident")
         make_identity(nc, ident[:])
@@ -78,46 +80,22 @@ def tile_attend_grwadam_pl_kernel(tc, xT, G, mT, v, offs, out_0, out_1, out_2, o
         nc.gpsimd.memset(one[:], 1.0)
         nv_cols = keep.tile([P, P], F32, name="nv_cols")
         nc.gpsimd.memset(nv_cols[:], 0.0)
+        nc.gpsimd.memset(up_windows[1][:], 0.0)
 
         warm = keep.tile([P, 1], F32, name="warm")
         nc.scalar.activation(out=warm[:], in_=one[:], func=ACT.Abs_reciprocal_sqrt)
-        factors = keep.tile([P, 2 * SLOTS], F32, name="factors")
+        factors = keep.tile([P, 3 * SLOTS], F32, name="factors")
         rate = factors[:, :SLOTS]
-        beta_early = factors[:, SLOTS:]
         beta_late = factors[:, SLOTS - 1 : 2 * SLOTS - 1]
-        nc.scalar.activation(out=beta_early, in_=one[:].to_broadcast([P, SLOTS]), func=ACT.Copy, scale=BETA1)
-
-        v_table = keep.tile([P, COLS], F32, name="v_table")
-        v_lines = v_table[:].rearrange("m (p a j) -> m a p j", a=blocks, j=RUN)
-        for a in range(blocks):
-            spread = sq_ps.tile([P, RUN, P], F32, name=f"spread{a}", tag=f"bank{a}")
-            for j in range(RUN):
-                column = v_row[:, RUN * a + j : RUN * a + j + 1]
-                nc.tensor.transpose(spread[:, j, :], column.to_broadcast([P, P]), ident[:])
-            nc.scalar.copy(out=v_lines[:, a], in_=spread[:].rearrange("m j p -> m p j"))
-
-        g_bf = keep.tile([P, SLOTS, PACK], BF16, name="g_bf", align_bytes=64)
-        nc.vector.tensor_copy(
-            out=g_bf[:].rearrange("p (c i) j -> p c j i", i=RUN),
-            in_=g_raw[:].rearrange("p j (c i) -> p c j i", i=RUN),
-        )
-        g_codes = keep.tile([P, SLOTS], U32, name="g_codes", align_bytes=64)
-        g_scales = keep.tile([P, SLOTS], U8, name="g_scales", align_bytes=64)
-        nc.vector.quantize_mx(
-            out=g_codes[:].bitcast(E5M2), scales=g_scales[:], in_=g_bf[:].rearrange("p i j -> p (i j)")
+        beta_early = factors[:, 2 * SLOTS :]
+        nc.scalar.activation(
+            out=factors[:, SLOTS:], in_=one[:].to_broadcast([P, 2 * SLOTS]), func=ACT.Copy, scale=BETA1
         )
 
-        v_listed = keep.tile([P, SLOTS], F32, name="v_listed")
-        nc.vector.tensor_copy(v_listed[:], v_table[:].indirect(offsets[:]))
-
-        dw9 = [keep.tile([P, SLOTS], F32, name=f"dw9_{t}")[:] for t in range(PACK)]
-        moment = [keep.tile([P, SLOTS], F32, name=f"moment{t}")[:] for t in range(PACK)]
-
-        turned = [sq_ps.tile([P, PACK, P], F32, name=f"turned{b}", tag=f"bank{b}") for b in range(blocks)]
-
+        x_codes, x_scales = [], []
         for t in range(PACK):
             x_bf = keep.tile([P, 2, P, 2], BF16, name=f"x_bf{t}")
-            cast = nc.scalar.copy if t < 3 else nc.vector.tensor_copy
+            cast = nc.scalar.copy if t < 2 else nc.vector.tensor_copy
             cast(out=x_bf[:], in_=x_raw[t][:].rearrange("m (p u e) -> m u p e", u=2, e=2))
             x_words = x_bf[:].rearrange("m u p e -> m (u p e)").bitcast(F32)
             x_turned = turn_ps.tile([P, 2, P], F32, name="x_turned", tag="turn")
@@ -128,20 +106,48 @@ def tile_attend_grwadam_pl_kernel(tc, xT, G, mT, v, offs, out_0, out_1, out_2, o
                 out=x_grouped[:].bitcast(F32).rearrange("p (m u) -> p m u", u=2),
                 in_=x_turned[:].rearrange("p u m -> p m u"),
             )
-            x_codes = keep.tile([P, P], U32, name=f"x_codes{t}", align_bytes=64)
-            x_scales = keep.tile([P, P], U8, name=f"x_scales{t}", align_bytes=64)
-            nc.vector.quantize_mx(out=x_codes[:].bitcast(E4M3), scales=x_scales[:], in_=x_grouped[:])
+            x_codes.append(keep.tile([P, P], U32, name=f"x_codes{t}", align_bytes=64))
+            x_scales.append(keep.tile([P, P], U8, name=f"x_scales{t}", align_bytes=64))
+            nc.vector.quantize_mx(out=x_codes[t][:].bitcast(E4M3), scales=x_scales[t][:], in_=x_grouped[:])
+
+        v_table = keep.tile([P, COLS], F32, name="v_table")
+        v_lines = v_table[:].rearrange("m (p a j) -> m a p j", a=blocks, j=RUN)
+        for a in range(blocks):
+            spread = sq_ps.tile([P, RUN, P], F32, name=f"spread{a}", tag=f"bank{a}")
+            for j in range(RUN):
+                column = v_row[:, RUN * a + j : RUN * a + j + 1]
+                nc.tensor.transpose(spread[:, j, :], column.to_broadcast([P, P]), ident[:])
+            nc.scalar.copy(out=v_lines[:, a], in_=spread[:].rearrange("m j p -> m p j"))
+
+        g_codes = keep.tile([P, SLOTS], U32, name="g_codes", align_bytes=64)
+        g_scales = keep.tile([P, SLOTS], U8, name="g_scales", align_bytes=64)
+        for h in range(2):
+            half = slice(h * SLOTS // 2, (h + 1) * SLOTS // 2)
+            g_bf = keep.tile([P, SLOTS // 2, PACK], BF16, name=f"g_bf{h}", align_bytes=64)
+            nc.vector.tensor_copy(out=g_bf[:], in_=g_raw[h][:].rearrange("p j i -> p i j"))
+            nc.vector.quantize_mx(
+                out=g_codes[:, half].bitcast(E5M2), scales=g_scales[:, half], in_=g_bf[:].rearrange("p i j -> p (i j)")
+            )
+
+        v_listed = keep.tile([P, SLOTS], F32, name="v_listed")
+        nc.vector.tensor_copy(v_listed[:], v_table[:].indirect(offsets[:]))
+
+        dw9 = [keep.tile([P, SLOTS], F32, name=f"dw9_{t}")[:] for t in range(PACK)]
+        moment = [keep.tile([P, SLOTS], F32, name="moment0")[:], beta_early, dw9[1], dw9[2]]
+        turned = [sq_ps.tile([P, PACK, P], F32, name=f"turned{b}", tag=f"bank{b}") for b in range(blocks)]
+        for t in range(PACK):
             dw = dw_ps.tile([P, SLOTS], F32, name="dw", tag="dw")
             nc.tensor.matmul_mx(
                 out=dw[:],
-                lhsT=x_codes[:].bitcast(E4M3),
-                lhsT_scale=x_scales[:],
+                lhsT=x_codes[t][:].bitcast(E4M3),
+                lhsT_scale=x_scales[t][:],
                 rhs=g_codes[:].bitcast(E5M2),
                 rhs_scale=g_scales[:],
                 start=True,
                 stop=True,
             )
             nc.scalar.activation(out=dw9[t], in_=dw[:], func=ACT.Copy, scale=DW_SCALE)
+        for t in range(PACK):
             for b in range(blocks):
                 nc.tensor.transpose(turned[b][:, t, :], dw9[t][:, b * P : (b + 1) * P], ident[:])
 
@@ -151,6 +157,11 @@ def tile_attend_grwadam_pl_kernel(tc, xT, G, mT, v, offs, out_0, out_1, out_2, o
         def scatter_moment(t, window, beta):
             nc.vector.tensor_tensor(window[:].indirect(offsets[:]), moment[t], beta, ALU.mult)
             nc.sync.dma_start(out=nm_rows[t], in_=window[:])
+
+        def late_window(name):
+            window = wide.tile([P, COLS], F32, name=name, tag="wide")
+            nc.gpsimd.memset(window[:], 0.0)
+            return window
 
         gather_moment(0)
         scatter_moment(0, nm_windows[0], beta_early)
@@ -199,6 +210,8 @@ def tile_attend_grwadam_pl_kernel(tc, xT, G, mT, v, offs, out_0, out_1, out_2, o
 
         for t in range(1, PACK):
             gather_moment(t)
+        up_windows.append(late_window("up_window2"))
+        nm_windows.append(late_window("nm_window1"))
 
         rounded = [keep.tile([P, PACK, PIECE], BF16, name=f"rounded{k}") for k in range(pieces)]
         grouped = [keep.tile([P, PIECE, PACK], BF16, name=f"grouped{k}", align_bytes=64) for k in range(pieces)]
@@ -210,11 +223,11 @@ def tile_attend_grwadam_pl_kernel(tc, xT, G, mT, v, offs, out_0, out_1, out_2, o
                 nc.scalar.copy(out=rounded[k][:, t, :], in_=window[:, k * PIECE : (k + 1) * PIECE])
                 if t == PACK - 1:
                     nc.scalar.copy(
-                        out=grouped[k][:].rearrange("p (c i) t -> p c t i", i=RUN),
-                        in_=rounded[k][:].rearrange("p t (c i) -> p c t i", i=RUN),
+                        out=grouped[k][:],
+                        in_=rounded[k][:].rearrange("p t c -> p c t"),
                     )
 
-        nc.vector.tensor_copy(out=beta_late[:, 0:1], in_=beta_early[:, 0:1])
+        nc.vector.tensor_copy(out=beta_late[:, 0:1], in_=beta_late[:, 1:2])
         for t in range(1, PACK):
             scatter_moment(t, nm_windows[t % len(nm_windows)], beta_late)
 

@@ -47,8 +47,7 @@ def tile_attend_grwadam_pl_kernel(tc, xT, G, mT, v, offs, out_0, out_1, out_2, o
     with ExitStack() as ctx:
         keep = ctx.enter_context(tc.tile_pool(name="keep", bufs=1))
         wide = ctx.enter_context(tc.tile_pool(name="wide", bufs=PACK))
-        turn_ps = ctx.enter_context(tc.psum_pool(name="turn_ps", bufs=2))
-        dw_ps = ctx.enter_context(tc.psum_pool(name="dw_ps", bufs=2))
+        turn_ps = ctx.enter_context(tc.psum_pool(name="turn_ps", bufs=4))
         sq_ps = ctx.enter_context(tc.psum_pool(name="sq_ps", bufs=1))
 
         offsets = keep.tile([P, SLOTS // 16], U16, name="offsets")
@@ -57,12 +56,13 @@ def tile_attend_grwadam_pl_kernel(tc, xT, G, mT, v, offs, out_0, out_1, out_2, o
         v_row = keep.tile([P, COLS // P], F32, name="v_row")
         nc.sync.dma_start(out=v_row[:], in_=v[0].rearrange("(p j) -> p j", p=P))
         x_raw = [keep.tile([P, R], F32, name=f"x_raw{t}") for t in range(PACK)]
-        for t in range(PACK):
-            nc.sync.dma_start(out=x_raw[t][:], in_=x_rows[t])
+        nc.sync.dma_start(out=x_raw[0][:], in_=x_rows[0])
         g_rows = G.rearrange("(p j) (h i) -> h p j i", j=PACK, h=2)
-        g_raw = [keep.tile([P, PACK, SLOTS // 2], F32, name=f"g_raw{h}") for h in range(2)]
+        g_raw = [keep.tile([P, PACK, SLOTS // 2], F32, name=f"g_raw{h}", tag=f"g_raw{h}") for h in range(2)]
         for h in range(2):
             nc.sync.dma_start(out=g_raw[h][:], in_=g_rows[h])
+        for t in range(1, PACK):
+            nc.sync.dma_start(out=x_raw[t][:], in_=x_rows[t])
         m_table = []
         for t in range(PACK):
             tile = wide.tile([P, COLS], F32, name=f"m_table{t}", tag="wide")
@@ -70,9 +70,7 @@ def tile_attend_grwadam_pl_kernel(tc, xT, G, mT, v, offs, out_0, out_1, out_2, o
             m_table.append(tile)
 
         nm_windows = [keep.tile([P, COLS], F32, name="nm_window0")]
-        up_windows = [keep.tile([P, COLS], F32, name=f"up_window{k}") for k in range(2)]
         nc.vector.memset(nm_windows[0][:], 0.0)
-        nc.vector.memset(up_windows[0][:], 0.0)
 
         ident = keep.tile([P, P], F32, name="ident")
         make_identity(nc, ident[:])
@@ -80,7 +78,6 @@ def tile_attend_grwadam_pl_kernel(tc, xT, G, mT, v, offs, out_0, out_1, out_2, o
         nc.gpsimd.memset(one[:], 1.0)
         nv_cols = keep.tile([P, P], F32, name="nv_cols")
         nc.gpsimd.memset(nv_cols[:], 0.0)
-        nc.gpsimd.memset(up_windows[1][:], 0.0)
 
         warm = keep.tile([P, 1], F32, name="warm")
         nc.scalar.activation(out=warm[:], in_=one[:], func=ACT.Abs_reciprocal_sqrt)
@@ -92,12 +89,28 @@ def tile_attend_grwadam_pl_kernel(tc, xT, G, mT, v, offs, out_0, out_1, out_2, o
             out=factors[:, SLOTS:], in_=one[:].to_broadcast([P, 2 * SLOTS]), func=ACT.Copy, scale=BETA1
         )
 
-        x_codes, x_scales = [], []
-        for t in range(PACK):
-            x_bf = keep.tile([P, 2, P, 2], BF16, name=f"x_bf{t}")
-            cast = nc.scalar.copy if t < 2 else nc.vector.tensor_copy
-            cast(out=x_bf[:], in_=x_raw[t][:].rearrange("m (p u e) -> m u p e", u=2, e=2))
-            x_words = x_bf[:].rearrange("m u p e -> m (u p e)").bitcast(F32)
+        v_table = keep.tile([P, COLS], F32, name="v_table")
+        v_lines = v_table[:].rearrange("m (p a j) -> m a p j", a=blocks, j=RUN)
+
+        def spread_v(a):
+            spread = sq_ps.tile([P, RUN, P], F32, name=f"spread{a}", tag=f"bank{a}")
+            for j in range(RUN):
+                column = v_row[:, RUN * a + j : RUN * a + j + 1]
+                nc.tensor.transpose(spread[:, j, :], column.to_broadcast([P, P]), ident[:])
+            nc.scalar.copy(out=v_lines[:, a], in_=spread[:].rearrange("m j p -> m p j"))
+
+        for a in range(blocks // 2):
+            spread_v(a)
+
+        x_codes = [keep.tile([P, P], U32, name=f"x_codes{t}", align_bytes=64) for t in range(PACK)]
+        x_scales = [keep.tile([P, P], U8, name=f"x_scales{t}", align_bytes=64) for t in range(PACK)]
+
+        def quantise_x(t, x_bf):
+            nc.vector.tensor_copy(
+                out=x_bf.rearrange("m (u p e) -> m u p e", u=2, e=2),
+                in_=x_raw[t][:].rearrange("m (p u e) -> m u p e", u=2, e=2),
+            )
+            x_words = x_bf.bitcast(F32)
             x_turned = turn_ps.tile([P, 2, P], F32, name="x_turned", tag="turn")
             for u in range(2):
                 nc.tensor.transpose(x_turned[:, u, :], x_words[:, u * P : (u + 1) * P], ident[:])
@@ -106,37 +119,36 @@ def tile_attend_grwadam_pl_kernel(tc, xT, G, mT, v, offs, out_0, out_1, out_2, o
                 out=x_grouped[:].bitcast(F32).rearrange("p (m u) -> p m u", u=2),
                 in_=x_turned[:].rearrange("p u m -> p m u"),
             )
-            x_codes.append(keep.tile([P, P], U32, name=f"x_codes{t}", align_bytes=64))
-            x_scales.append(keep.tile([P, P], U8, name=f"x_scales{t}", align_bytes=64))
             nc.vector.quantize_mx(out=x_codes[t][:].bitcast(E4M3), scales=x_scales[t][:], in_=x_grouped[:])
 
-        v_table = keep.tile([P, COLS], F32, name="v_table")
-        v_lines = v_table[:].rearrange("m (p a j) -> m a p j", a=blocks, j=RUN)
-        for a in range(blocks):
-            spread = sq_ps.tile([P, RUN, P], F32, name=f"spread{a}", tag=f"bank{a}")
-            for j in range(RUN):
-                column = v_row[:, RUN * a + j : RUN * a + j + 1]
-                nc.tensor.transpose(spread[:, j, :], column.to_broadcast([P, P]), ident[:])
-            nc.scalar.copy(out=v_lines[:, a], in_=spread[:].rearrange("m j p -> m p j"))
+        x_bf_first = keep.tile([P, R], BF16, name="x_bf_first")
+        quantise_x(0, x_bf_first[:])
+
+        for a in range(blocks // 2, blocks):
+            spread_v(a)
 
         g_codes = keep.tile([P, SLOTS], U32, name="g_codes", align_bytes=64)
         g_scales = keep.tile([P, SLOTS], U8, name="g_scales", align_bytes=64)
         for h in range(2):
             half = slice(h * SLOTS // 2, (h + 1) * SLOTS // 2)
-            g_bf = keep.tile([P, SLOTS // 2, PACK], BF16, name=f"g_bf{h}", align_bytes=64)
+            g_bf = keep.tile([P, SLOTS // 2, PACK], BF16, name=f"g_bf{h}", tag="g_bf", align_bytes=64)
             nc.vector.tensor_copy(out=g_bf[:], in_=g_raw[h][:].rearrange("p j i -> p i j"))
             nc.vector.quantize_mx(
                 out=g_codes[:, half].bitcast(E5M2), scales=g_scales[:, half], in_=g_bf[:].rearrange("p i j -> p (i j)")
             )
 
-        v_listed = keep.tile([P, SLOTS], F32, name="v_listed")
+        x_bf_rest = keep.tile([P, (PACK - 1) * R], BF16, name="x_bf_rest", tag="g_raw1")
+        for t in range(1, PACK):
+            quantise_x(t, x_bf_rest[:, (t - 1) * R : t * R])
+
+        v_listed = keep.tile([P, SLOTS], F32, name="v_listed", tag="g_bf", align_bytes=64)
         nc.vector.tensor_copy(v_listed[:], v_table[:].indirect(offsets[:]))
 
-        dw9 = [keep.tile([P, SLOTS], F32, name=f"dw9_{t}")[:] for t in range(PACK)]
+        dw9 = [keep.tile([P, SLOTS], F32, name=f"dw9_{t}", tag=f"dw9_{t}", align_bytes=64)[:] for t in range(PACK)]
         moment = [keep.tile([P, SLOTS], F32, name="moment0")[:], beta_early, dw9[1], dw9[2]]
         turned = [sq_ps.tile([P, PACK, P], F32, name=f"turned{b}", tag=f"bank{b}") for b in range(blocks)]
         for t in range(PACK):
-            dw = dw_ps.tile([P, SLOTS], F32, name="dw", tag="dw")
+            dw = turn_ps.tile([P, SLOTS], F32, name="dw", tag="turn")
             nc.tensor.matmul_mx(
                 out=dw[:],
                 lhsT=x_codes[t][:].bitcast(E4M3),
@@ -210,7 +222,7 @@ def tile_attend_grwadam_pl_kernel(tc, xT, G, mT, v, offs, out_0, out_1, out_2, o
 
         for t in range(1, PACK):
             gather_moment(t)
-        up_windows.append(late_window("up_window2"))
+        up_windows = [late_window(f"up_window{k}") for k in range(3)]
         nm_windows.append(late_window("nm_window1"))
 
         rounded = [keep.tile([P, PACK, PIECE], BF16, name=f"rounded{k}") for k in range(pieces)]
@@ -231,20 +243,21 @@ def tile_attend_grwadam_pl_kernel(tc, xT, G, mT, v, offs, out_0, out_1, out_2, o
         for t in range(1, PACK):
             scatter_moment(t, nm_windows[t % len(nm_windows)], beta_late)
 
-        up_codes = keep.tile([P, COLS], U32, name="up_codes", align_bytes=64)
-        up_scales = keep.tile([P, COLS], U8, name="up_scales", align_bytes=64)
+        up_scales = keep.tile([P, PIECE], U8, name="up_scales", align_bytes=64)
         words = out_3[0].rearrange("p c j -> p (c j)").bitcast(I32)
         for k in range(pieces):
             cols = slice(k * PIECE, (k + 1) * PIECE)
+            tag = "dw9_2" if k == 2 else f"up_codes{k}"
+            up_codes = keep.tile([P, PIECE], U32, name=f"up_codes{k}", tag=tag, align_bytes=64)
             nc.vector.quantize_mx(
-                out=up_codes[:, cols].bitcast(E4M3),
-                scales=up_scales[:, cols],
+                out=up_codes[:].bitcast(E4M3),
+                scales=up_scales[4 * k : P, :],
                 in_=grouped[k][:].rearrange("p c t -> p (c t)"),
             )
-            nc.sync.dma_start(out=words[:, cols], in_=up_codes[:, cols].bitcast(I32))
+            nc.sync.dma_start(out=words[:, cols], in_=up_codes[:].bitcast(I32))
         scale_rows = out_4[0].bitcast(I32)
         for quad in range(4):
             nc.scalar.dma_start(
-                out=scale_rows[4 * quad : 4 * quad + 4, :],
-                in_=up_scales[32 * quad : 32 * quad + 4, :].bitcast(I32),
+                out=scale_rows[4 * quad : 4 * quad + 4, :].rearrange("j (k c) -> k j c", k=pieces),
+                in_=up_scales[32 * quad : 32 * quad + 4 * pieces, :].bitcast(I32),
             )

@@ -17,18 +17,25 @@ ALU = mybir.AluOpType
 
 P = 128
 PACK = 4
+QUADRANT = 32
+SCALE_ROWS = 4
 D = 512
 R = 512
 SLOTS = 512
 COLS = 2048
+BLOCKS = SLOTS // P
+V_RUN = 4
+G_PARTS = 2
 PIECE = 512
-RUN = 4
+PIECES = COLS // PIECE
+WORK_BANKS = 4
+UP_WINDOWS = 3
 
 BETA1 = 0.9
 BETA2 = 0.99
 EPS = 0.001
 DW_SCALE = (1.0 - BETA1) / BETA1
-TINY = 1e-30
+GUARD = 1e-14
 
 FLOPS = 2 * D * R * SLOTS
 BYTES = 4 * (D * R + R * SLOTS + D * COLS + COLS + 2 * D * COLS + SLOTS) + 2 * P * SLOTS // 16 + D * COLS + 16 * COLS
@@ -36,19 +43,17 @@ BYTES = 4 * (D * R + R * SLOTS + D * COLS + COLS + 2 * D * COLS + SLOTS) + 2 * P
 
 def tile_attend_grwadam_pl_kernel(tc, xT, G, mT, v, offs, out_0, out_1, out_2, out_3, out_4):
     nc = tc.nc
-    blocks = SLOTS // P
-    pieces = COLS // PIECE
 
-    x_rows = xT.rearrange("(p t) r -> t p r", t=PACK)
-    m_rows = mT.rearrange("(p t) c -> t p c", t=PACK)
-    up_rows = out_0.rearrange("(p t) c -> t p c", t=PACK)
-    nm_rows = out_1.rearrange("(p t) c -> t p c", t=PACK)
+    x_lanes = xT.rearrange("(p t) r -> t p r", t=PACK)
+    m_lanes = mT.rearrange("(p t) c -> t p c", t=PACK)
+    up_lanes = out_0.rearrange("(p t) c -> t p c", t=PACK)
+    nm_lanes = out_1.rearrange("(p t) c -> t p c", t=PACK)
 
     with ExitStack() as ctx:
         keep = ctx.enter_context(tc.tile_pool(name="keep", bufs=1))
         wide = ctx.enter_context(tc.tile_pool(name="wide", bufs=PACK))
-        turn_ps = ctx.enter_context(tc.psum_pool(name="turn_ps", bufs=4))
-        sq_ps = ctx.enter_context(tc.psum_pool(name="sq_ps", bufs=1))
+        work_ps = ctx.enter_context(tc.psum_pool(name="work_ps", bufs=WORK_BANKS))
+        named_ps = ctx.enter_context(tc.psum_pool(name="named_ps", bufs=1))
 
         offsets = keep.tile([P, SLOTS // 16], U16, name="offsets")
         nc.sync.dma_start(offsets[:], offs)
@@ -56,21 +61,24 @@ def tile_attend_grwadam_pl_kernel(tc, xT, G, mT, v, offs, out_0, out_1, out_2, o
         v_row = keep.tile([P, COLS // P], F32, name="v_row")
         nc.sync.dma_start(out=v_row[:], in_=v[0].rearrange("(p j) -> p j", p=P))
         x_raw = [keep.tile([P, R], F32, name=f"x_raw{t}") for t in range(PACK)]
-        nc.sync.dma_start(out=x_raw[0][:], in_=x_rows[0])
-        g_rows = G.rearrange("(p j) (h i) -> h p j i", j=PACK, h=2)
-        g_raw = [keep.tile([P, PACK, SLOTS // 2], F32, name=f"g_raw{h}", tag=f"g_raw{h}") for h in range(2)]
-        for h in range(2):
-            nc.sync.dma_start(out=g_raw[h][:], in_=g_rows[h])
+        nc.sync.dma_start(out=x_raw[0][:], in_=x_lanes[0])
+        g_parts = G.rearrange("(p j) (h i) -> h p j i", j=PACK, h=G_PARTS)
+        g_raw = [
+            keep.tile([P, PACK, SLOTS // G_PARTS], F32, name=f"g_raw{h}", tag=f"g_raw{h}") for h in range(G_PARTS)
+        ]
+        for h in range(G_PARTS):
+            nc.sync.dma_start(out=g_raw[h][:], in_=g_parts[h])
         for t in range(1, PACK):
-            nc.sync.dma_start(out=x_raw[t][:], in_=x_rows[t])
+            nc.sync.dma_start(out=x_raw[t][:], in_=x_lanes[t])
         m_table = []
         for t in range(PACK):
-            tile = wide.tile([P, COLS], F32, name=f"m_table{t}", tag="wide")
-            nc.sync.dma_start(out=tile[:], in_=m_rows[t])
-            m_table.append(tile)
+            m_lane = wide.tile([P, COLS], F32, name=f"m_table{t}", tag="wide")
+            nc.sync.dma_start(out=m_lane[:], in_=m_lanes[t])
+            m_table.append(m_lane)
 
-        nm_windows = [keep.tile([P, COLS], F32, name="nm_window0")]
-        nc.vector.memset(nm_windows[0][:], 0.0)
+        nm_windows = [keep.tile([P, COLS], F32, name=f"nm_window{k}") for k in range(2)]
+        for window in nm_windows:
+            nc.vector.memset(window[:], 0.0)
 
         ident = keep.tile([P, P], F32, name="ident")
         make_identity(nc, ident[:])
@@ -79,8 +87,9 @@ def tile_attend_grwadam_pl_kernel(tc, xT, G, mT, v, offs, out_0, out_1, out_2, o
         nv_cols = keep.tile([P, P], F32, name="nv_cols")
         nc.gpsimd.memset(nv_cols[:], 0.0)
 
-        warm = keep.tile([P, 1], F32, name="warm")
-        nc.scalar.activation(out=warm[:], in_=one[:], func=ACT.Abs_reciprocal_sqrt)
+        guard = keep.tile([P, 1], F32, name="guard")
+        nc.scalar.activation(out=guard[:], in_=one[:], func=ACT.Abs_reciprocal_sqrt, scale=1.0 / (GUARD * GUARD))
+
         factors = keep.tile([P, 3 * SLOTS], F32, name="factors")
         rate = factors[:, :SLOTS]
         beta_late = factors[:, SLOTS - 1 : 2 * SLOTS - 1]
@@ -90,16 +99,17 @@ def tile_attend_grwadam_pl_kernel(tc, xT, G, mT, v, offs, out_0, out_1, out_2, o
         )
 
         v_table = keep.tile([P, COLS], F32, name="v_table")
-        v_lines = v_table[:].rearrange("m (p a j) -> m a p j", a=blocks, j=RUN)
+        v_groups = COLS // P // V_RUN
+        v_runs = v_table[:].rearrange("m (p a j) -> m a p j", a=v_groups, j=V_RUN)
 
         def spread_v(a):
-            spread = sq_ps.tile([P, RUN, P], F32, name=f"spread{a}", tag=f"bank{a}")
-            for j in range(RUN):
-                column = v_row[:, RUN * a + j : RUN * a + j + 1]
+            spread = named_ps.tile([P, V_RUN, P], F32, name=f"spread{a}", tag=f"bank{a}")
+            for j in range(V_RUN):
+                column = v_row[:, V_RUN * a + j : V_RUN * a + j + 1]
                 nc.tensor.transpose(spread[:, j, :], column.to_broadcast([P, P]), ident[:])
-            nc.scalar.copy(out=v_lines[:, a], in_=spread[:].rearrange("m j p -> m p j"))
+            nc.scalar.copy(out=v_runs[:, a], in_=spread[:].rearrange("m j p -> m p j"))
 
-        for a in range(blocks // 2):
+        for a in range(v_groups // 2):
             spread_v(a)
 
         x_codes = [keep.tile([P, P], U32, name=f"x_codes{t}", align_bytes=64) for t in range(PACK)]
@@ -110,10 +120,10 @@ def tile_attend_grwadam_pl_kernel(tc, xT, G, mT, v, offs, out_0, out_1, out_2, o
                 out=x_bf.rearrange("m (u p e) -> m u p e", u=2, e=2),
                 in_=x_raw[t][:].rearrange("m (p u e) -> m u p e", u=2, e=2),
             )
-            x_words = x_bf.bitcast(F32)
-            x_turned = turn_ps.tile([P, 2, P], F32, name="x_turned", tag="turn")
+            x_pairs = x_bf.bitcast(F32)
+            x_turned = work_ps.tile([P, 2, P], F32, name="x_turned", tag="work")
             for u in range(2):
-                nc.tensor.transpose(x_turned[:, u, :], x_words[:, u * P : (u + 1) * P], ident[:])
+                nc.tensor.transpose(x_turned[:, u, :], x_pairs[:, u * P : (u + 1) * P], ident[:])
             x_grouped = keep.tile([P, P * PACK], BF16, name=f"x_grouped{t}", align_bytes=64)
             nc.scalar.copy(
                 out=x_grouped[:].bitcast(F32).rearrange("p (m u) -> p m u", u=2),
@@ -124,31 +134,31 @@ def tile_attend_grwadam_pl_kernel(tc, xT, G, mT, v, offs, out_0, out_1, out_2, o
         x_bf_first = keep.tile([P, R], BF16, name="x_bf_first")
         quantise_x(0, x_bf_first[:])
 
-        for a in range(blocks // 2, blocks):
+        for a in range(v_groups // 2, v_groups):
             spread_v(a)
 
         g_codes = keep.tile([P, SLOTS], U32, name="g_codes", align_bytes=64)
         g_scales = keep.tile([P, SLOTS], U8, name="g_scales", align_bytes=64)
-        for h in range(2):
-            half = slice(h * SLOTS // 2, (h + 1) * SLOTS // 2)
-            g_bf = keep.tile([P, SLOTS // 2, PACK], BF16, name=f"g_bf{h}", tag="g_bf", align_bytes=64)
+        for h in range(G_PARTS):
+            part = slice(h * SLOTS // G_PARTS, (h + 1) * SLOTS // G_PARTS)
+            g_bf = keep.tile([P, SLOTS // G_PARTS, PACK], BF16, name=f"g_bf{h}", tag="g_bf", align_bytes=64)
             nc.vector.tensor_copy(out=g_bf[:], in_=g_raw[h][:].rearrange("p j i -> p i j"))
             nc.vector.quantize_mx(
-                out=g_codes[:, half].bitcast(E5M2), scales=g_scales[:, half], in_=g_bf[:].rearrange("p i j -> p (i j)")
+                out=g_codes[:, part].bitcast(E5M2), scales=g_scales[:, part], in_=g_bf[:].rearrange("p i j -> p (i j)")
             )
 
-        x_bf_rest = keep.tile([P, (PACK - 1) * R], BF16, name="x_bf_rest", tag="g_raw1")
+        x_bf_rest = keep.tile([P, (PACK - 1) * R], BF16, name="x_bf_rest", tag=f"g_raw{G_PARTS - 1}")
         for t in range(1, PACK):
             quantise_x(t, x_bf_rest[:, (t - 1) * R : t * R])
 
         v_listed = keep.tile([P, SLOTS], F32, name="v_listed", tag="g_bf", align_bytes=64)
         nc.vector.tensor_copy(v_listed[:], v_table[:].indirect(offsets[:]))
 
-        dw9 = [keep.tile([P, SLOTS], F32, name=f"dw9_{t}", tag=f"dw9_{t}", align_bytes=64)[:] for t in range(PACK)]
-        moment = [keep.tile([P, SLOTS], F32, name="moment0")[:], beta_early, dw9[1], dw9[2]]
-        turned = [sq_ps.tile([P, PACK, P], F32, name=f"turned{b}", tag=f"bank{b}") for b in range(blocks)]
+        dw_scaled = [keep.tile([P, SLOTS], F32, name=f"dw_scaled{t}")[:] for t in range(PACK)]
+        moment = [keep.tile([P, SLOTS], F32, name="moment0")[:], beta_early, dw_scaled[1], dw_scaled[2]]
+        dw_turned = [named_ps.tile([P, PACK, P], F32, name=f"dw_turned{b}", tag=f"bank{b}") for b in range(BLOCKS)]
         for t in range(PACK):
-            dw = turn_ps.tile([P, SLOTS], F32, name="dw", tag="turn")
+            dw = work_ps.tile([P, SLOTS], F32, name="dw", tag="work")
             nc.tensor.matmul_mx(
                 out=dw[:],
                 lhsT=x_codes[t][:].bitcast(E4M3),
@@ -158,17 +168,18 @@ def tile_attend_grwadam_pl_kernel(tc, xT, G, mT, v, offs, out_0, out_1, out_2, o
                 start=True,
                 stop=True,
             )
-            nc.scalar.activation(out=dw9[t], in_=dw[:], func=ACT.Copy, scale=DW_SCALE)
+            nc.scalar.activation(out=dw_scaled[t], in_=dw[:], func=ACT.Copy, scale=DW_SCALE)
         for t in range(PACK):
-            for b in range(blocks):
-                nc.tensor.transpose(turned[b][:, t, :], dw9[t][:, b * P : (b + 1) * P], ident[:])
+            for b in range(BLOCKS):
+                nc.tensor.transpose(dw_turned[b][:, t, :], dw_scaled[t][:, b * P : (b + 1) * P], ident[:])
 
         def gather_moment(t):
-            nc.vector.tensor_tensor(moment[t], m_table[t][:].indirect(offsets[:]), dw9[t], ALU.add)
+            nc.vector.tensor_tensor(moment[t], m_table[t][:].indirect(offsets[:]), dw_scaled[t], ALU.add)
 
-        def scatter_moment(t, window, beta):
+        def scatter_nm(t, beta):
+            window = nm_windows[t % (PACK - 1)]
             nc.vector.tensor_tensor(window[:].indirect(offsets[:]), moment[t], beta, ALU.mult)
-            nc.sync.dma_start(out=nm_rows[t], in_=window[:])
+            nc.sync.dma_start(out=nm_lanes[t], in_=window[:])
 
         def late_window(name):
             window = wide.tile([P, COLS], F32, name=name, tag="wide")
@@ -176,32 +187,32 @@ def tile_attend_grwadam_pl_kernel(tc, xT, G, mT, v, offs, out_0, out_1, out_2, o
             return window
 
         gather_moment(0)
-        scatter_moment(0, nm_windows[0], beta_early)
+        scatter_nm(0, beta_early)
 
-        v_turned = turn_ps.tile([P, blocks, P], F32, name="v_turned", tag="turn")
-        for b in range(blocks):
+        v_turned = work_ps.tile([P, BLOCKS, P], F32, name="v_turned", tag="work")
+        for b in range(BLOCKS):
             nc.tensor.transpose(v_turned[:, b, :], v_listed[:, b * P : (b + 1) * P], ident[:])
-        v_cols = keep.tile([P, blocks], F32, name="v_cols")
+        v_cols = keep.tile([P, BLOCKS], F32, name="v_cols")
         nc.scalar.activation(out=v_cols[:], in_=v_turned[:, :, 0], func=ACT.Copy, scale=BETA2)
 
-        q_cols = keep.tile([P, blocks], F32, name="q_cols")
-        squares = keep.tile([P, D], F32, name="squares")
-        rsqrt = keep.tile([P, blocks], F32, name="rsqrt")
-        denom2 = keep.tile([P, blocks], F32, name="denom2")
-        rate_cols = keep.tile([P, blocks], F32, name="rate_cols")
-        sq_scale = math.sqrt((1.0 - BETA2) / D) / DW_SCALE
-        for b in range(blocks):
+        q_cols = keep.tile([P, BLOCKS], F32, name="q_cols")
+        squares = keep.tile([P, BLOCKS * D], F32, name="squares")
+        rsqrt = keep.tile([P, BLOCKS], F32, name="rsqrt")
+        denom2 = keep.tile([P, BLOCKS], F32, name="denom2")
+        rate_cols = keep.tile([P, BLOCKS], F32, name="rate_cols")
+        square_scale = math.sqrt((1.0 - BETA2) / D) / DW_SCALE
+        for b in range(BLOCKS):
             col = slice(b, b + 1)
             nc.scalar.activation(
-                out=squares[:],
-                in_=turned[b][:].rearrange("i t p -> i (t p)"),
+                out=squares[:, b * D : (b + 1) * D],
+                in_=dw_turned[b][:].rearrange("i t p -> i (t p)"),
                 func=ACT.Square,
-                scale=sq_scale,
+                scale=square_scale,
                 accum_out=q_cols[:, col],
             )
             nc.scalar.activation(out=nv_cols[:, col], in_=q_cols[:, col], func=ACT.Identity, bias=v_cols[:, col])
-        nc.scalar.activation(out=rsqrt[:], in_=nv_cols[:, :blocks], func=ACT.Abs_reciprocal_sqrt, bias=TINY)
-        for b in range(blocks):
+        nc.scalar.activation(out=rsqrt[:], in_=nv_cols[:, :BLOCKS], func=ACT.Abs_reciprocal_sqrt, bias=guard[:])
+        for b in range(BLOCKS):
             col = slice(b, b + 1)
             nc.scalar.activation(
                 out=denom2[:, col], in_=nv_cols[:, col], func=ACT.Square, scale=rsqrt[:, col], bias=EPS
@@ -209,55 +220,50 @@ def tile_attend_grwadam_pl_kernel(tc, xT, G, mT, v, offs, out_0, out_1, out_2, o
         nc.scalar.activation(
             out=rate_cols[:], in_=denom2[:], func=ACT.Abs_reciprocal_sqrt, scale=1.0 / (BETA1 * BETA1)
         )
-        rate_ps = turn_ps.tile([P, blocks, P], F32, name="rate_ps", tag="turn")
-        for b in range(blocks):
+        rate_ps = work_ps.tile([P, BLOCKS, P], F32, name="rate_ps", tag="work")
+        for b in range(BLOCKS):
             nc.tensor.transpose(rate_ps[:, b, :], rate_cols[:, b : b + 1].to_broadcast([P, P]), ident[:])
         nc.scalar.copy(out=rate, in_=rate_ps[:].rearrange("p b i -> p (b i)"))
 
-        nv_ps = turn_ps.tile([P, P], F32, name="nv_ps", tag="turn")
+        nv_ps = work_ps.tile([P, P], F32, name="nv_ps", tag="work")
         nc.tensor.transpose(nv_ps[:], nv_cols[:], ident[:])
-        nv_rows = keep.tile([32, P], F32, name="nv_rows")
-        nc.scalar.copy(out=nv_rows[:], in_=nv_ps[0:32, :])
-        nc.sync.dma_start(out=out_2.rearrange("o (b i) -> (o b) i", b=blocks), in_=nv_rows[0:blocks, :])
+        nv_rows = keep.tile([QUADRANT, P], F32, name="nv_rows")
+        nc.scalar.copy(out=nv_rows[:], in_=nv_ps[0:QUADRANT, :])
+        nc.sync.dma_start(out=out_2.rearrange("o (b i) -> (o b) i", b=BLOCKS), in_=nv_rows[0:BLOCKS, :])
 
         for t in range(1, PACK):
             gather_moment(t)
-        up_windows = [late_window(f"up_window{k}") for k in range(3)]
-        nm_windows.append(late_window("nm_window1"))
+        up_windows = [late_window(f"up_window{k}") for k in range(UP_WINDOWS)]
+        nm_windows.append(late_window("nm_window2"))
 
-        rounded = [keep.tile([P, PACK, PIECE], BF16, name=f"rounded{k}") for k in range(pieces)]
-        grouped = [keep.tile([P, PIECE, PACK], BF16, name=f"grouped{k}", align_bytes=64) for k in range(pieces)]
+        rounded = [keep.tile([P, PACK, PIECE], BF16, name=f"rounded{k}") for k in range(PIECES)]
+        grouped = [keep.tile([P, PIECE, PACK], BF16, name=f"grouped{k}", align_bytes=64) for k in range(PIECES)]
         for t in range(PACK):
-            window = up_windows[t % len(up_windows)]
+            window = up_windows[t % UP_WINDOWS]
             nc.vector.tensor_tensor(window[:].indirect(offsets[:]), moment[t], rate, ALU.mult)
-            nc.sync.dma_start(out=up_rows[t], in_=window[:])
-            for k in range(pieces):
+            nc.sync.dma_start(out=up_lanes[t], in_=window[:])
+            for k in range(PIECES):
                 nc.scalar.copy(out=rounded[k][:, t, :], in_=window[:, k * PIECE : (k + 1) * PIECE])
                 if t == PACK - 1:
-                    nc.scalar.copy(
-                        out=grouped[k][:],
-                        in_=rounded[k][:].rearrange("p t c -> p c t"),
-                    )
+                    nc.scalar.copy(out=grouped[k][:], in_=rounded[k][:].rearrange("p t c -> p c t"))
 
         nc.vector.tensor_copy(out=beta_late[:, 0:1], in_=beta_late[:, 1:2])
         for t in range(1, PACK):
-            scatter_moment(t, nm_windows[t % len(nm_windows)], beta_late)
+            scatter_nm(t, beta_late)
 
         up_scales = keep.tile([P, PIECE], U8, name="up_scales", align_bytes=64)
         words = out_3[0].rearrange("p c j -> p (c j)").bitcast(I32)
-        for k in range(pieces):
-            cols = slice(k * PIECE, (k + 1) * PIECE)
-            tag = "dw9_2" if k == 2 else f"up_codes{k}"
-            up_codes = keep.tile([P, PIECE], U32, name=f"up_codes{k}", tag=tag, align_bytes=64)
+        for k in range(PIECES):
+            up_codes = keep.tile([P, PIECE], U32, name=f"up_codes{k}", align_bytes=64)
             nc.vector.quantize_mx(
                 out=up_codes[:].bitcast(E4M3),
-                scales=up_scales[4 * k : P, :],
+                scales=up_scales[SCALE_ROWS * k : P, :],
                 in_=grouped[k][:].rearrange("p c t -> p (c t)"),
             )
-            nc.sync.dma_start(out=words[:, cols], in_=up_codes[:].bitcast(I32))
+            nc.sync.dma_start(out=words[:, k * PIECE : (k + 1) * PIECE], in_=up_codes[:].bitcast(I32))
         scale_rows = out_4[0].bitcast(I32)
-        for quad in range(4):
+        for quad in range(P // QUADRANT):
             nc.scalar.dma_start(
-                out=scale_rows[4 * quad : 4 * quad + 4, :].rearrange("j (k c) -> k j c", k=pieces),
-                in_=up_scales[32 * quad : 32 * quad + 4 * pieces, :].bitcast(I32),
+                out=scale_rows[SCALE_ROWS * quad : SCALE_ROWS * (quad + 1), :].rearrange("j (k c) -> k j c", k=PIECES),
+                in_=up_scales[QUADRANT * quad : QUADRANT * quad + SCALE_ROWS * PIECES, :].bitcast(I32),
             )

from contextlib import ExitStack
import math

import concourse.mybir as mybir
from concourse.masks import make_identity

F32 = mybir.dt.float32
BF16 = mybir.dt.bfloat16
U32 = mybir.dt.uint32
I32 = mybir.dt.int32
U16 = mybir.dt.uint16
U8 = mybir.dt.uint8
E4M3 = mybir.dt.float8_e4m3fn_x4
E5M2 = mybir.dt.float8_e5m2_x4
ACT = mybir.ActivationFunctionType
ALU = mybir.AluOpType

P = 128
PACK = 4
QUADRANT = 32
SCALE_ROWS = 4
D = 512
R = 512
SLOTS = 512
COLS = 2048
BLOCKS = SLOTS // P
V_RUN = 4
G_PARTS = 2
PIECE = 512
PIECES = COLS // PIECE
WORK_BANKS = 4
UP_WINDOWS = 3

BETA1 = 0.9
BETA2 = 0.99
EPS = 0.001
DW_SCALE = (1.0 - BETA1) / BETA1
GUARD = 1e-14

FLOPS = 2 * D * R * SLOTS
BYTES = 4 * (D * R + R * SLOTS + D * COLS + COLS + 2 * D * COLS + SLOTS) + 2 * P * SLOTS // 16 + D * COLS + 16 * COLS


def tile_attend_grwadam_pl_kernel(tc, xT, G, mT, v, offs, out_0, out_1, out_2, out_3, out_4):
    nc = tc.nc

    x_lanes = xT.rearrange("(p t) r -> t p r", t=PACK)
    m_lanes = mT.rearrange("(p t) c -> t p c", t=PACK)
    up_lanes = out_0.rearrange("(p t) c -> t p c", t=PACK)
    nm_lanes = out_1.rearrange("(p t) c -> t p c", t=PACK)

    with ExitStack() as ctx:
        keep = ctx.enter_context(tc.tile_pool(name="keep", bufs=1))
        wide = ctx.enter_context(tc.tile_pool(name="wide", bufs=PACK))
        work_ps = ctx.enter_context(tc.psum_pool(name="work_ps", bufs=WORK_BANKS))
        named_ps = ctx.enter_context(tc.psum_pool(name="named_ps", bufs=1))

        offsets = keep.tile([P, SLOTS // 16], U16, name="offsets")
        nc.sync.dma_start(offsets[:], offs)

        v_row = keep.tile([P, COLS // P], F32, name="v_row")
        nc.sync.dma_start(out=v_row[:], in_=v[0].rearrange("(p j) -> p j", p=P))
        x_raw = [keep.tile([P, R], F32, name=f"x_raw{t}") for t in range(PACK)]
        nc.sync.dma_start(out=x_raw[0][:], in_=x_lanes[0])
        g_parts = G.rearrange("(p j) (h i) -> h p j i", j=PACK, h=G_PARTS)
        g_raw = [
            keep.tile([P, PACK, SLOTS // G_PARTS], F32, name=f"g_raw{h}", tag=f"g_raw{h}") for h in range(G_PARTS)
        ]
        for h in range(G_PARTS):
            nc.sync.dma_start(out=g_raw[h][:], in_=g_parts[h])
        for t in range(1, PACK):
            nc.sync.dma_start(out=x_raw[t][:], in_=x_lanes[t])
        m_table = []
        for t in range(PACK):
            m_lane = wide.tile([P, COLS], F32, name=f"m_table{t}", tag="wide")
            nc.sync.dma_start(out=m_lane[:], in_=m_lanes[t])
            m_table.append(m_lane)

        nm_windows = [keep.tile([P, COLS], F32, name=f"nm_window{k}") for k in range(2)]
        for window in nm_windows:
            nc.vector.memset(window[:], 0.0)

        ident = keep.tile([P, P], F32, name="ident")
        make_identity(nc, ident[:])
        one = keep.tile([P, 1], F32, name="one")
        nc.gpsimd.memset(one[:], 1.0)
        nv_cols = keep.tile([P, P], F32, name="nv_cols")
        nc.gpsimd.memset(nv_cols[:], 0.0)

        guard = keep.tile([P, 1], F32, name="guard")
        nc.scalar.activation(out=guard[:], in_=one[:], func=ACT.Abs_reciprocal_sqrt, scale=1.0 / (GUARD * GUARD))

        factors = keep.tile([P, 3 * SLOTS], F32, name="factors")
        rate = factors[:, :SLOTS]
        beta_late = factors[:, SLOTS - 1 : 2 * SLOTS - 1]
        beta_early = factors[:, 2 * SLOTS :]
        nc.scalar.activation(
            out=factors[:, SLOTS:], in_=one[:].to_broadcast([P, 2 * SLOTS]), func=ACT.Copy, scale=BETA1
        )

        v_table = keep.tile([P, COLS], F32, name="v_table")
        v_groups = COLS // P // V_RUN
        v_runs = v_table[:].rearrange("m (p a j) -> m a p j", a=v_groups, j=V_RUN)

        def spread_v(a):
            spread = named_ps.tile([P, V_RUN, P], F32, name=f"spread{a}", tag=f"bank{a}")
            for j in range(V_RUN):
                column = v_row[:, V_RUN * a + j : V_RUN * a + j + 1]
                nc.tensor.transpose(spread[:, j, :], column.to_broadcast([P, P]), ident[:])
            nc.scalar.copy(out=v_runs[:, a], in_=spread[:].rearrange("m j p -> m p j"))

        for a in range(v_groups // 2):
            spread_v(a)

        x_codes = [keep.tile([P, P], U32, name=f"x_codes{t}", align_bytes=64) for t in range(PACK)]
        x_scales = [keep.tile([P, P], U8, name=f"x_scales{t}", align_bytes=64) for t in range(PACK)]

        def quantise_x(t, x_bf):
            nc.vector.tensor_copy(
                out=x_bf.rearrange("m (u p e) -> m u p e", u=2, e=2),
                in_=x_raw[t][:].rearrange("m (p u e) -> m u p e", u=2, e=2),
            )
            x_pairs = x_bf.bitcast(F32)
            x_turned = work_ps.tile([P, 2, P], F32, name="x_turned", tag="work")
            for u in range(2):
                nc.tensor.transpose(x_turned[:, u, :], x_pairs[:, u * P : (u + 1) * P], ident[:])
            x_grouped = keep.tile([P, P * PACK], BF16, name=f"x_grouped{t}", align_bytes=64)
            nc.scalar.copy(
                out=x_grouped[:].bitcast(F32).rearrange("p (m u) -> p m u", u=2),
                in_=x_turned[:].rearrange("p u m -> p m u"),
            )
            nc.vector.quantize_mx(out=x_codes[t][:].bitcast(E4M3), scales=x_scales[t][:], in_=x_grouped[:])

        x_bf_first = keep.tile([P, R], BF16, name="x_bf_first")
        quantise_x(0, x_bf_first[:])

        for a in range(v_groups // 2, v_groups):
            spread_v(a)

        g_codes = keep.tile([P, SLOTS], U32, name="g_codes", align_bytes=64)
        g_scales = keep.tile([P, SLOTS], U8, name="g_scales", align_bytes=64)
        for h in range(G_PARTS):
            part = slice(h * SLOTS // G_PARTS, (h + 1) * SLOTS // G_PARTS)
            g_bf = keep.tile([P, SLOTS // G_PARTS, PACK], BF16, name=f"g_bf{h}", tag="g_bf", align_bytes=64)
            nc.vector.tensor_copy(out=g_bf[:], in_=g_raw[h][:].rearrange("p j i -> p i j"))
            nc.vector.quantize_mx(
                out=g_codes[:, part].bitcast(E5M2), scales=g_scales[:, part], in_=g_bf[:].rearrange("p i j -> p (i j)")
            )

        x_bf_rest = keep.tile([P, (PACK - 1) * R], BF16, name="x_bf_rest", tag=f"g_raw{G_PARTS - 1}")
        for t in range(1, PACK):
            quantise_x(t, x_bf_rest[:, (t - 1) * R : t * R])

        v_listed = keep.tile([P, SLOTS], F32, name="v_listed", tag="g_bf", align_bytes=64)
        nc.vector.tensor_copy(v_listed[:], v_table[:].indirect(offsets[:]))

        dw_scaled = [keep.tile([P, SLOTS], F32, name=f"dw_scaled{t}")[:] for t in range(PACK)]
        moment = [keep.tile([P, SLOTS], F32, name="moment0")[:], beta_early, dw_scaled[1], dw_scaled[2]]
        dw_turned = [named_ps.tile([P, PACK, P], F32, name=f"dw_turned{b}", tag=f"bank{b}") for b in range(BLOCKS)]
        for t in range(PACK):
            dw = work_ps.tile([P, SLOTS], F32, name="dw", tag="work")
            nc.tensor.matmul_mx(
                out=dw[:],
                lhsT=x_codes[t][:].bitcast(E4M3),
                lhsT_scale=x_scales[t][:],
                rhs=g_codes[:].bitcast(E5M2),
                rhs_scale=g_scales[:],
                start=True,
                stop=True,
            )
            nc.scalar.activation(out=dw_scaled[t], in_=dw[:], func=ACT.Copy, scale=DW_SCALE)
        for t in range(PACK):
            for b in range(BLOCKS):
                nc.tensor.transpose(dw_turned[b][:, t, :], dw_scaled[t][:, b * P : (b + 1) * P], ident[:])

        def gather_moment(t):
            nc.vector.tensor_tensor(moment[t], m_table[t][:].indirect(offsets[:]), dw_scaled[t], ALU.add)

        def scatter_nm(t, beta):
            window = nm_windows[t % (PACK - 1)]
            nc.vector.tensor_tensor(window[:].indirect(offsets[:]), moment[t], beta, ALU.mult)
            nc.sync.dma_start(out=nm_lanes[t], in_=window[:])

        def late_window(name):
            window = wide.tile([P, COLS], F32, name=name, tag="wide")
            nc.gpsimd.memset(window[:], 0.0)
            return window

        gather_moment(0)
        scatter_nm(0, beta_early)

        v_turned = work_ps.tile([P, BLOCKS, P], F32, name="v_turned", tag="work")
        for b in range(BLOCKS):
            nc.tensor.transpose(v_turned[:, b, :], v_listed[:, b * P : (b + 1) * P], ident[:])
        v_cols = keep.tile([P, BLOCKS], F32, name="v_cols")
        nc.scalar.activation(out=v_cols[:], in_=v_turned[:, :, 0], func=ACT.Copy, scale=BETA2)

        q_cols = keep.tile([P, BLOCKS], F32, name="q_cols")
        squares = keep.tile([P, BLOCKS * D], F32, name="squares")
        rsqrt = keep.tile([P, BLOCKS], F32, name="rsqrt")
        denom2 = keep.tile([P, BLOCKS], F32, name="denom2")
        rate_cols = keep.tile([P, BLOCKS], F32, name="rate_cols")
        square_scale = math.sqrt((1.0 - BETA2) / D) / DW_SCALE
        for b in range(BLOCKS):
            col = slice(b, b + 1)
            nc.scalar.activation(
                out=squares[:, b * D : (b + 1) * D],
                in_=dw_turned[b][:].rearrange("i t p -> i (t p)"),
                func=ACT.Square,
                scale=square_scale,
                accum_out=q_cols[:, col],
            )
            nc.scalar.activation(out=nv_cols[:, col], in_=q_cols[:, col], func=ACT.Identity, bias=v_cols[:, col])
        nc.scalar.activation(out=rsqrt[:], in_=nv_cols[:, :BLOCKS], func=ACT.Abs_reciprocal_sqrt, bias=guard[:])
        for b in range(BLOCKS):
            col = slice(b, b + 1)
            nc.scalar.activation(
                out=denom2[:, col], in_=nv_cols[:, col], func=ACT.Square, scale=rsqrt[:, col], bias=EPS
            )
        nc.scalar.activation(
            out=rate_cols[:], in_=denom2[:], func=ACT.Abs_reciprocal_sqrt, scale=1.0 / (BETA1 * BETA1)
        )
        rate_ps = work_ps.tile([P, BLOCKS, P], F32, name="rate_ps", tag="work")
        for b in range(BLOCKS):
            nc.tensor.transpose(rate_ps[:, b, :], rate_cols[:, b : b + 1].to_broadcast([P, P]), ident[:])
        nc.scalar.copy(out=rate, in_=rate_ps[:].rearrange("p b i -> p (b i)"))

        nv_ps = work_ps.tile([P, P], F32, name="nv_ps", tag="work")
        nc.tensor.transpose(nv_ps[:], nv_cols[:], ident[:])
        nv_rows = keep.tile([QUADRANT, P], F32, name="nv_rows")
        nc.scalar.copy(out=nv_rows[:], in_=nv_ps[0:QUADRANT, :])
        nc.sync.dma_start(out=out_2.rearrange("o (b i) -> (o b) i", b=BLOCKS), in_=nv_rows[0:BLOCKS, :])

        for t in range(1, PACK):
            gather_moment(t)
        up_windows = [late_window(f"up_window{k}") for k in range(UP_WINDOWS)]
        nm_windows.append(late_window("nm_window2"))

        rounded = [keep.tile([P, PACK, PIECE], BF16, name=f"rounded{k}") for k in range(PIECES)]
        grouped = [keep.tile([P, PIECE, PACK], BF16, name=f"grouped{k}", align_bytes=64) for k in range(PIECES)]
        for t in range(PACK):
            window = up_windows[t % UP_WINDOWS]
            nc.vector.tensor_tensor(window[:].indirect(offsets[:]), moment[t], rate, ALU.mult)
            nc.sync.dma_start(out=up_lanes[t], in_=window[:])
            for k in range(PIECES):
                nc.scalar.copy(out=rounded[k][:, t, :], in_=window[:, k * PIECE : (k + 1) * PIECE])
                if t == PACK - 1:
                    nc.scalar.copy(out=grouped[k][:], in_=rounded[k][:].rearrange("p t c -> p c t"))

        nc.vector.tensor_copy(out=beta_late[:, 0:1], in_=beta_late[:, 1:2])
        for t in range(1, PACK):
            scatter_nm(t, beta_late)

        up_scales = keep.tile([P, PIECE], U8, name="up_scales", align_bytes=64)
        words = out_3[0].rearrange("p c j -> p (c j)").bitcast(I32)
        for k in range(PIECES):
            up_codes = keep.tile([P, PIECE], U32, name=f"up_codes{k}", align_bytes=64)
            nc.vector.quantize_mx(
                out=up_codes[:].bitcast(E4M3),
                scales=up_scales[SCALE_ROWS * k : P, :],
                in_=grouped[k][:].rearrange("p c t -> p (c t)"),
            )
            nc.sync.dma_start(out=words[:, k * PIECE : (k + 1) * PIECE], in_=up_codes[:].bitcast(I32))
        scale_rows = out_4[0].bitcast(I32)
        for quad in range(P // QUADRANT):
            nc.scalar.dma_start(
                out=scale_rows[SCALE_ROWS * quad : SCALE_ROWS * (quad + 1), :].rearrange("j (k c) -> k j c", k=PIECES),
                in_=up_scales[QUADRANT * quad : QUADRANT * quad + SCALE_ROWS * PIECES, :].bitcast(I32),
            )
